import numpy as np
import ml_dtypes


def mxq(x, axis, fmt="e4m3"):
    dtype, down = {"e4m3": (ml_dtypes.float8_e4m3fn, 7), "e5m2": (ml_dtypes.float8_e5m2, 14)}[fmt]
    v = np.moveaxis(np.asarray(x, np.float32).astype(ml_dtypes.bfloat16).astype(np.float64), axis, -1)
    blocks = v.reshape(v.shape[:-1] + (-1, 32))
    amax = np.abs(blocks).max(-1, keepdims=True)
    byte = np.maximum(np.where(amax > 0, np.frexp(amax)[1] - 1 + 127, 0) - down, 1)
    scale = np.exp2(byte - 127.0)
    codes = (blocks / scale).astype(np.float32).astype(dtype).astype(np.float64)
    return np.moveaxis((codes * scale).reshape(v.shape), -1, axis)


WIDE = False


def mx_kscale(k):
    if not WIDE:
        return np.ones(k)
    levels = np.array([10, -10, 5, -5, 0])
    if k % 512:
        return np.exp2(np.random.permutation(np.resize(levels, k // 32))).repeat(32)
    a = np.empty((k // 512, 16))
    for p in range(k // 512):
        a[p, :8] = np.random.permutation(np.resize(levels, 8))
        for g in range(8):
            far = levels[np.abs(levels - a[p, g]) >= 10]
            a[p, g + 8] = far[np.random.randint(len(far))]
    return np.exp2(a.ravel()).repeat(32)


def f64(x):
    return np.asarray(x).astype(np.float64)


def striped(idx):
    return np.tile(np.asarray(idx).reshape(-1, 16).T, (8, 1)).astype(np.uint16)


def unstriped(offs):
    return offs[:16].T.reshape(-1).astype(np.int64)


E2M1 = np.array([0.0, 0.5, 1.0, 1.5, 2.0, 3.0, 4.0, 6.0, -0.0, -0.5, -1.0, -1.5, -2.0, -3.0, -4.0, -6.0])


def pack_weight(w, fmt):
    k, n = w.shape
    w = f64(np.asarray(w, np.float32).astype(ml_dtypes.bfloat16)).reshape(k // 32, 32, n)
    amax = np.abs(w).max(1)
    if fmt == "e4m3":
        byte = np.frexp(amax)[1] - 1 + 127 - 7
    else:
        mant, ex = np.frexp(amax / 6.0)
        byte = np.where(mant > 0.5, ex, ex - 1) + 127
    byte = np.clip(np.where(amax > 0, byte, 1), 1, 254)
    scaled = (w * np.exp2(127.0 - byte)[:, None, :]).reshape(k, n).astype(np.float32)
    by_word = np.ascontiguousarray(scaled.reshape(k // 512, 128, 4, n).transpose(0, 1, 3, 2))
    if fmt == "e4m3":
        words = by_word.astype(ml_dtypes.float8_e4m3fn).view(np.uint8)
    else:
        c = by_word.astype(ml_dtypes.float4_e2m1fn).view(np.uint8) & 0xF
        words = (c[..., 0::2] | (c[..., 1::2] << 4)).reshape(k // 512, 128, 2 * n)
    return np.ascontiguousarray(words), np.ascontiguousarray(byte.astype(np.uint8).reshape(k // 512, 16, n))


def unpack_weight(words, scales, fmt):
    g, _, n = scales.shape
    words = np.ascontiguousarray(words).reshape(g, 128, n, -1)
    if fmt == "e4m3":
        vals = words.view(ml_dtypes.float8_e4m3fn).astype(np.float64)
    else:
        nib = np.empty((g, 128, n, 4), np.uint8)
        nib[..., 0::2] = words & 0xF
        nib[..., 1::2] = words >> 4
        vals = E2M1[nib]
    vals = vals * np.repeat(np.exp2(scales.astype(np.float64) - 127.0), 8, axis=1)[..., None]
    return vals.transpose(0, 1, 3, 2).reshape(g * 512, n)


B, N, T, D, NQ = 1, 512, 2048, 1024, 128


def setup_inputs():
    n = np.random.standard_normal
    idx = np.random.permutation(T)[:B * N]
    s = mx_kscale(D)[:, None]
    kp = pack_weight(n((D, T)) / s, "e2m1")
    cp = pack_weight(n((D, T)) / s, "e2m1")
    return {
        "qT": (n((B, D, NQ)) * s * (1.00 / np.sqrt(D))).astype(np.float32),
        "k_words": np.ascontiguousarray(kp[0].reshape(1, 2, 128, T, 2).transpose(0, 2, 3, 1, 4)).reshape(1, 128, T, 4),
        "k_scales": kp[1],
        "c_words": np.ascontiguousarray(cp[0].reshape(1, 2, 128, T, 2).transpose(0, 2, 3, 1, 4)).reshape(1, 128, T, 4),
        "c_scales": cp[1],
        "offs": striped(idx),
    }


def reference(qT, k_words, k_scales, c_words, c_scales, offs):
    idx = unstriped(offs)
    pick = lambda x, which: x[:, which].reshape(x.shape[0], B, -1).transpose(1, 0, 2)
    k = unpack_weight(k_words.reshape(1, 128, T, 2, 2).transpose(0, 3, 1, 2, 4).reshape(2, 128, 2 * T), k_scales, "e2m1")
    kg = pick(k, idx)
    c = unpack_weight(c_words.reshape(1, 128, T, 2, 2).transpose(0, 3, 1, 2, 4).reshape(2, 128, 2 * T), c_scales, "e2m1")
    cg = pick(c, idx)
    qq = mxq(f64(qT), 1, "e4m3")
    a = qq.transpose(0, 2, 1) @ kg
    z = qq.transpose(0, 2, 1) @ cg
    y = np.log(1.0 + np.maximum(a * z, 0.0))
    return y

@@ -1,0 +1,121 @@
+from contextlib import ExitStack
+
+import concourse.mybir as mybir
+
+F32 = mybir.dt.float32
+BF16 = mybir.dt.bfloat16
+I32 = mybir.dt.int32
+U32 = mybir.dt.uint32
+U16 = mybir.dt.uint16
+U8 = mybir.dt.uint8
+FP8X4 = mybir.dt.float8_e4m3fn_x4
+FP4X4 = mybir.dt.float4_e2m1fn_x4
+ALU = mybir.AluOpType
+ACT = mybir.ActivationFunctionType
+
+P = 128
+N, T, D, NQ = 512, 2048, 1024, 128
+PASSES = 2
+PACK = 4
+HALF = N // 2
+GROUP = 128
+SHIFT = 4
+MOVED = 112
+FLOPS = 2 * 2 * NQ * N * D
+
+
+def tile_attend_bilin_topk_kernel(tc, qT, k_words, k_scales, c_words, c_scales, offs, out):
+    nc = tc.nc
+    with ExitStack() as ctx:
+        keep = ctx.enter_context(tc.tile_pool(name="keep", bufs=1))
+        psum = ctx.enter_context(tc.psum_pool(name="psum", bufs=1))
+
+        offsets = keep.tile([P, N // 16], U16, name="offsets")
+        nc.sync.dma_start(offsets[:], offs)
+
+        ks_win = keep.tile([P, T // 4], I32, name="ks_win", align_bytes=64)
+        cs_win = keep.tile([P, T // 4], I32, name="cs_win", align_bytes=64)
+        nc.vector.memset(ks_win[:], 0)
+        nc.gpsimd.memset(cs_win[:], 0)
+        for q in range(4):
+            nc.sync.dma_start(ks_win[32 * q : 32 * q + 8, :], k_scales[:, 4 * q : 4 * q + 4, :].bitcast(I32))
+        for q in range(4):
+            nc.gpsimd.dma_start(cs_win[32 * q : 32 * q + 8, :], c_scales[:, 4 * q : 4 * q + 4, :].bitcast(I32))
+
+        q_raw = keep.tile([P, PASSES, PACK, NQ], F32, name="q_raw")
+        nc.sync.dma_start(q_raw[:], qT[0].rearrange("(o p j) m -> p o j m", o=PASSES, j=PACK))
+        kw_win = keep.tile([P, T], I32, name="kw_win", align_bytes=64)
+        nc.sync.dma_start(kw_win[:], k_words[0].rearrange("p t b -> p (t b)").bitcast(I32))
+        cw_win = keep.tile([P, T], I32, name="cw_win", align_bytes=64)
+        nc.sync.dma_start(cw_win[:], c_words[0].rearrange("p t b -> p (t b)").bitcast(I32))
+
+        one = keep.tile([P, 1], F32, name="one")
+        nc.vector.memset(one[:], 1.0)
+        warm = keep.tile([P, 1], F32, name="warm")
+        nc.scalar.activation(out=warm[:], in_=one[:], func=ACT.Ln)
+
+        ks1 = keep.tile([P, N // 4], I32, name="ks1", align_bytes=64)
+        cs1 = keep.tile([P, N // 4], I32, name="cs1", align_bytes=64)
+        nc.vector.memset(ks1[:], 0)
+        nc.vector.memset(cs1[:], 0)
+
+        ks0 = keep.tile([P, N], U8, name="ks0", align_bytes=64)
+        nc.vector.tensor_copy(ks0[:], ks_win[:].bitcast(U8).indirect(offsets[:]))
+
+        q_bf = keep.tile([P, PASSES, NQ, PACK], BF16, name="q_bf", align_bytes=64)
+        nc.scalar.copy(out=q_bf[:], in_=q_raw[:].rearrange("p o j m -> p o m j"))
+        nc.scalar.dma_start(ks1[0:MOVED, :], ks0[SHIFT : SHIFT + MOVED, :].bitcast(I32))
+
+        q_codes = keep.tile([P, PASSES * NQ], U32, name="q_codes", align_bytes=64)
+        q_scale = keep.tile([P, PASSES * NQ], U8, name="q_scale", align_bytes=64)
+        nc.vector.quantize_mx(
+            out=q_codes[:].bitcast(FP8X4), scales=q_scale[:], in_=q_bf[:].rearrange("p o m j -> p (o m j)")
+        )
+
+        cs0 = keep.tile([P, N], U8, name="cs0", align_bytes=64)
+        nc.vector.tensor_copy(cs0[:], cs_win[:].bitcast(U8).indirect(offsets[:]))
+        nc.scalar.dma_start(cs1[0:MOVED, :], cs0[SHIFT : SHIFT + MOVED, :].bitcast(I32))
+
+        def product(acc, codes, planes, cols, scols):
+            for o in range(PASSES):
+                nc.tensor.matmul_mx(
+                    out=acc,
+                    lhsT=q_codes[:, o * NQ : (o + 1) * NQ].bitcast(FP8X4),
+                    lhsT_scale=q_scale[:, o * NQ : (o + 1) * NQ],
+                    rhs=codes[:, o, cols].bitcast(FP4X4),
+                    rhs_scale=planes[o][:, scols],
+                    start=(o == 0),
+                    stop=(o == PASSES - 1),
+                )
+
+        kg = keep.tile([P, N], U32, name="kg", align_bytes=64)
+        nc.vector.tensor_copy(kg[:], kw_win[:].bitcast(U32).indirect(offsets[:]))
+        k_codes = keep.tile([P, PASSES, N], U16, name="k_codes", align_bytes=64)
+        nc.vector.tensor_copy(k_codes[:], kg[:].bitcast(U16).rearrange("p (n o) -> p o n", o=PASSES))
+        a_ps = psum.tile([P, N], F32, name="a_ps")
+        product(a_ps[:], k_codes, [ks0[:], ks1[:].bitcast(U8)], slice(0, N), slice(0, N))
+        a_sb = keep.tile([P, N], F32, name="a_sb")
+        nc.scalar.copy(out=a_sb[:], in_=a_ps[:])
+
+        z_ps = []
+        for h in range(2):
+            cg = keep.tile([P, HALF], U32, name=f"cg{h}", align_bytes=64)
+            nc.vector.tensor_copy(cg[:], cw_win[:].bitcast(U32).indirect(offsets[:, 16 * h : 16 * (h + 1)]))
+            c_codes = keep.tile([P, PASSES, HALF], U16, name=f"c_codes{h}", align_bytes=64)
+            nc.vector.tensor_copy(c_codes[:], cg[:].bitcast(U16).rearrange("p (n o) -> p o n", o=PASSES))
+            for g in range(2):
+                z = psum.tile([P, GROUP], F32, name=f"z{h}{g}")
+                c0 = h * HALF + g * GROUP
+                product(z[:], c_codes, [cs0[:], cs1[:].bitcast(U8)], slice(g * GROUP, (g + 1) * GROUP), slice(c0, c0 + GROUP))
+                z_ps.append(z)
+
+        for h in range(2):
+            res = keep.tile([P, HALF], F32, name=f"res{h}")
+            for g in range(2):
+                c0 = h * HALF + g * GROUP
+                prod = keep.tile([P, GROUP], F32, name=f"prod{h}{g}")
+                nc.vector.tensor_tensor(prod[:], z_ps[2 * h + g][:], a_sb[:, c0 : c0 + GROUP], ALU.mult)
+                pos = keep.tile([P, GROUP], F32, name=f"pos{h}{g}")
+                nc.vector.tensor_scalar(pos[:], prod[:], 0.0, 1.0, ALU.max, ALU.add)
+                nc.scalar.activation(out=res[:, g * GROUP : (g + 1) * GROUP], in_=pos[:], func=ACT.Ln)
+            nc.sync.dma_start(out[0][:, h * HALF : (h + 1) * HALF], res[:])

@@ -19,8 +19,6 @@ PASSES = 2
 PACK = 4
 HALF = N // 2
 GROUP = 128
-SHIFT = 4
-MOVED = 112
 FLOPS = 2 * 2 * NQ * N * D
 
 
@@ -35,12 +33,10 @@ def tile_attend_bilin_topk_kernel(tc, qT, k_words, k_scales, c_words, c_scales, 
 
         ks_win = keep.tile([P, T // 4], I32, name="ks_win", align_bytes=64)
         cs_win = keep.tile([P, T // 4], I32, name="cs_win", align_bytes=64)
-        nc.vector.memset(ks_win[:], 0)
-        nc.gpsimd.memset(cs_win[:], 0)
-        for q in range(4):
-            nc.sync.dma_start(ks_win[32 * q : 32 * q + 8, :], k_scales[:, 4 * q : 4 * q + 4, :].bitcast(I32))
-        for q in range(4):
-            nc.gpsimd.dma_start(cs_win[32 * q : 32 * q + 8, :], c_scales[:, 4 * q : 4 * q + 4, :].bitcast(I32))
+        for win, scales in ((ks_win, k_scales), (cs_win, c_scales)):
+            rows = scales.rearrange("o (u v j) t -> v (o u) j t", u=2, v=2).bitcast(I32)
+            for v in range(2):
+                nc.sync.dma_start(win[48 + 32 * v : 64 + 32 * v, :], rows[v])
 
         q_raw = keep.tile([P, PASSES, PACK, NQ], F32, name="q_raw")
         nc.sync.dma_start(q_raw[:], qT[0].rearrange("(o p j) m -> p o j m", o=PASSES, j=PACK))
@@ -54,27 +50,35 @@ def tile_attend_bilin_topk_kernel(tc, qT, k_words, k_scales, c_words, c_scales, 
         warm = keep.tile([P, 1], F32, name="warm")
         nc.scalar.activation(out=warm[:], in_=one[:], func=ACT.Ln)
 
-        ks1 = keep.tile([P, N // 4], I32, name="ks1", align_bytes=64)
-        cs1 = keep.tile([P, N // 4], I32, name="cs1", align_bytes=64)
-        nc.vector.memset(ks1[:], 0)
-        nc.vector.memset(cs1[:], 0)
+        for win in (ks_win, cs_win):
+            for lo, hi in ((0, 48), (64, 80), (96, 128)):
+                nc.vector.memset(win[lo:hi, :], 0)
 
-        ks0 = keep.tile([P, N], U8, name="ks0", align_bytes=64)
-        nc.vector.tensor_copy(ks0[:], ks_win[:].bitcast(U8).indirect(offsets[:]))
+        def spread(queues, plane, gathered):
+            for o in range(PASSES):
+                for u in range(2):
+                    first = 48 + 8 * o + 4 * u
+                    queues[2 * o + u].dma_start(plane[64 * u : 64 * (u + 1), o, :], gathered[first : first + 64, :].bitcast(I32))
+
+        ksg = keep.tile([P, N], U8, name="ksg", align_bytes=64)
+        nc.vector.tensor_copy(ksg[:], ks_win[:].bitcast(U8).indirect(offsets[:]))
+        ks = keep.tile([P, PASSES, N // 4], I32, name="ks", align_bytes=64)
+        spread([nc.scalar] * 4, ks, ksg)
+
+        csg = keep.tile([P, N], U8, name="csg", align_bytes=64)
+        nc.vector.tensor_copy(csg[:], cs_win[:].bitcast(U8).indirect(offsets[:]))
+        cs = keep.tile([P, PASSES, N // 4], I32, name="cs", align_bytes=64)
+        spread([nc.gpsimd, nc.sync, nc.sync, nc.sync], cs, csg)
 
         q_bf = keep.tile([P, PASSES, NQ, PACK], BF16, name="q_bf", align_bytes=64)
-        nc.scalar.copy(out=q_bf[:], in_=q_raw[:].rearrange("p o j m -> p o m j"))
-        nc.scalar.dma_start(ks1[0:MOVED, :], ks0[SHIFT : SHIFT + MOVED, :].bitcast(I32))
+        for o in range(PASSES):
+            nc.scalar.copy(out=q_bf[:, o], in_=q_raw[:, o].rearrange("p j m -> p m j"))
 
         q_codes = keep.tile([P, PASSES * NQ], U32, name="q_codes", align_bytes=64)
         q_scale = keep.tile([P, PASSES * NQ], U8, name="q_scale", align_bytes=64)
         nc.vector.quantize_mx(
             out=q_codes[:].bitcast(FP8X4), scales=q_scale[:], in_=q_bf[:].rearrange("p o m j -> p (o m j)")
         )
-
-        cs0 = keep.tile([P, N], U8, name="cs0", align_bytes=64)
-        nc.vector.tensor_copy(cs0[:], cs_win[:].bitcast(U8).indirect(offsets[:]))
-        nc.scalar.dma_start(cs1[0:MOVED, :], cs0[SHIFT : SHIFT + MOVED, :].bitcast(I32))
 
         def product(acc, codes, planes, cols, scols):
             for o in range(PASSES):
@@ -83,7 +87,7 @@ def tile_attend_bilin_topk_kernel(tc, qT, k_words, k_scales, c_words, c_scales, 
                     lhsT=q_codes[:, o * NQ : (o + 1) * NQ].bitcast(FP8X4),
                     lhsT_scale=q_scale[:, o * NQ : (o + 1) * NQ],
                     rhs=codes[:, o, cols].bitcast(FP4X4),
-                    rhs_scale=planes[o][:, scols],
+                    rhs_scale=planes[:, o, :].bitcast(U8)[:, scols],
                     start=(o == 0),
                     stop=(o == PASSES - 1),
                 )
@@ -93,7 +97,7 @@ def tile_attend_bilin_topk_kernel(tc, qT, k_words, k_scales, c_words, c_scales, 
         k_codes = keep.tile([P, PASSES, N], U16, name="k_codes", align_bytes=64)
         nc.vector.tensor_copy(k_codes[:], kg[:].bitcast(U16).rearrange("p (n o) -> p o n", o=PASSES))
         a_ps = psum.tile([P, N], F32, name="a_ps")
-        product(a_ps[:], k_codes, [ks0[:], ks1[:].bitcast(U8)], slice(0, N), slice(0, N))
+        product(a_ps[:], k_codes, ks, slice(0, N), slice(0, N))
         a_sb = keep.tile([P, N], F32, name="a_sb")
         nc.scalar.copy(out=a_sb[:], in_=a_ps[:])
 
@@ -106,16 +110,18 @@ def tile_attend_bilin_topk_kernel(tc, qT, k_words, k_scales, c_words, c_scales, 
             for g in range(2):
                 z = psum.tile([P, GROUP], F32, name=f"z{h}{g}")
                 c0 = h * HALF + g * GROUP
-                product(z[:], c_codes, [cs0[:], cs1[:].bitcast(U8)], slice(g * GROUP, (g + 1) * GROUP), slice(c0, c0 + GROUP))
+                product(z[:], c_codes, cs, slice(g * GROUP, (g + 1) * GROUP), slice(c0, c0 + GROUP))
                 z_ps.append(z)
 
-        for h in range(2):
-            res = keep.tile([P, HALF], F32, name=f"res{h}")
-            for g in range(2):
-                c0 = h * HALF + g * GROUP
-                prod = keep.tile([P, GROUP], F32, name=f"prod{h}{g}")
-                nc.vector.tensor_tensor(prod[:], z_ps[2 * h + g][:], a_sb[:, c0 : c0 + GROUP], ALU.mult)
-                pos = keep.tile([P, GROUP], F32, name=f"pos{h}{g}")
-                nc.vector.tensor_scalar(pos[:], prod[:], 0.0, 1.0, ALU.max, ALU.add)
-                nc.scalar.activation(out=res[:, g * GROUP : (g + 1) * GROUP], in_=pos[:], func=ACT.Ln)
-            nc.sync.dma_start(out[0][:, h * HALF : (h + 1) * HALF], res[:])
+        res = keep.tile([P, N], F32, name="res")
+        stored = 0
+        for g in range(4):
+            cols = slice(g * GROUP, (g + 1) * GROUP)
+            prod = keep.tile([P, GROUP], F32, name=f"prod{g}")
+            nc.vector.tensor_tensor(prod[:], z_ps[g][:], a_sb[:, cols], ALU.mult)
+            pos = keep.tile([P, GROUP], F32, name=f"pos{g}")
+            nc.vector.tensor_scalar(pos[:], prod[:], 0.0, 1.0, ALU.max, ALU.add)
+            nc.scalar.activation(out=res[:, cols], in_=pos[:], func=ACT.Ln)
+            if g > 0:
+                nc.sync.dma_start(out[0][:, stored : cols.stop], res[:, stored : cols.stop])
+                stored = cols.stop

@@ -38,7 +38,7 @@ def tile_attend_bilin_topk_kernel(tc, qT, k_words, k_scales, c_words, c_scales, 
             for v in range(2):
                 nc.sync.dma_start(win[48 + 32 * v : 64 + 32 * v, :], rows[v])
 
-        q_raw = keep.tile([P, PASSES, PACK, NQ], F32, name="q_raw")
+        q_raw = keep.tile([P, PASSES, PACK, NQ], F32, name="q_raw", tag="q_then_ks", align_bytes=64)
         nc.sync.dma_start(q_raw[:], qT[0].rearrange("(o p j) m -> p o j m", o=PASSES, j=PACK))
         kw_win = keep.tile([P, T], I32, name="kw_win", align_bytes=64)
         nc.sync.dma_start(kw_win[:], k_words[0].rearrange("p t b -> p (t b)").bitcast(I32))
@@ -50,9 +50,12 @@ def tile_attend_bilin_topk_kernel(tc, qT, k_words, k_scales, c_words, c_scales, 
         warm = keep.tile([P, 1], F32, name="warm")
         nc.scalar.activation(out=warm[:], in_=one[:], func=ACT.Ln)
 
-        for win in (ks_win, cs_win):
+        for engine, win in ((nc.vector, ks_win), (nc.gpsimd, cs_win)):
             for lo, hi in ((0, 48), (64, 80), (96, 128)):
-                nc.vector.memset(win[lo:hi, :], 0)
+                engine.memset(win[lo:hi, :], 0)
+
+        q_bf = keep.tile([P, PASSES, NQ, PACK], BF16, name="q_bf", align_bytes=64)
+        nc.scalar.copy(out=q_bf[:], in_=q_raw[:].rearrange("p o j m -> p o m j"))
 
         def spread(queues, plane, gathered):
             for o in range(PASSES):
@@ -62,17 +65,13 @@ def tile_attend_bilin_topk_kernel(tc, qT, k_words, k_scales, c_words, c_scales, 
 
         ksg = keep.tile([P, N], U8, name="ksg", align_bytes=64)
         nc.vector.tensor_copy(ksg[:], ks_win[:].bitcast(U8).indirect(offsets[:]))
-        ks = keep.tile([P, PASSES, N // 4], I32, name="ks", align_bytes=64)
+        ks = keep.tile([P, PASSES, N // 4], I32, name="ks", tag="q_then_ks", align_bytes=64)
         spread([nc.scalar] * 4, ks, ksg)
 
         csg = keep.tile([P, N], U8, name="csg", align_bytes=64)
         nc.vector.tensor_copy(csg[:], cs_win[:].bitcast(U8).indirect(offsets[:]))
         cs = keep.tile([P, PASSES, N // 4], I32, name="cs", align_bytes=64)
-        spread([nc.gpsimd, nc.sync, nc.sync, nc.sync], cs, csg)
-
-        q_bf = keep.tile([P, PASSES, NQ, PACK], BF16, name="q_bf", align_bytes=64)
-        for o in range(PASSES):
-            nc.scalar.copy(out=q_bf[:, o], in_=q_raw[:, o].rearrange("p j m -> p m j"))
+        spread([nc.sync] * 4, cs, csg)
 
         q_codes = keep.tile([P, PASSES * NQ], U32, name="q_codes", align_bytes=64)
         q_scale = keep.tile([P, PASSES * NQ], U8, name="q_scale", align_bytes=64)
@@ -96,32 +95,49 @@ def tile_attend_bilin_topk_kernel(tc, qT, k_words, k_scales, c_words, c_scales, 
         nc.vector.tensor_copy(kg[:], kw_win[:].bitcast(U32).indirect(offsets[:]))
         k_codes = keep.tile([P, PASSES, N], U16, name="k_codes", align_bytes=64)
         nc.vector.tensor_copy(k_codes[:], kg[:].bitcast(U16).rearrange("p (n o) -> p o n", o=PASSES))
-        a_ps = psum.tile([P, N], F32, name="a_ps")
-        product(a_ps[:], k_codes, ks, slice(0, N), slice(0, N))
         a_sb = keep.tile([P, N], F32, name="a_sb")
-        nc.scalar.copy(out=a_sb[:], in_=a_ps[:])
-
-        z_ps = []
         for h in range(2):
-            cg = keep.tile([P, HALF], U32, name=f"cg{h}", align_bytes=64)
-            nc.vector.tensor_copy(cg[:], cw_win[:].bitcast(U32).indirect(offsets[:, 16 * h : 16 * (h + 1)]))
-            c_codes = keep.tile([P, PASSES, HALF], U16, name=f"c_codes{h}", align_bytes=64)
-            nc.vector.tensor_copy(c_codes[:], cg[:].bitcast(U16).rearrange("p (n o) -> p o n", o=PASSES))
-            for g in range(2):
-                z = psum.tile([P, GROUP], F32, name=f"z{h}{g}")
-                c0 = h * HALF + g * GROUP
-                product(z[:], c_codes, cs, slice(g * GROUP, (g + 1) * GROUP), slice(c0, c0 + GROUP))
-                z_ps.append(z)
+            a_ps = psum.tile([P, HALF], F32, name=f"a_ps{h}")
+            for g0 in range(0, HALF, GROUP):
+                cols = slice(h * HALF + g0, h * HALF + g0 + GROUP)
+                product(a_ps[:, g0 : g0 + GROUP], k_codes, ks, cols, cols)
+            nc.scalar.copy(out=a_sb[:, h * HALF : (h + 1) * HALF], in_=a_ps[:])
+
+        cg = []
+        for h in range(2):
+            words = keep.tile([P, HALF], U32, name=f"cg{h}", align_bytes=64)
+            nc.vector.tensor_copy(words[:], cw_win[:].bitcast(U32).indirect(offsets[:, 16 * h : 16 * (h + 1)]))
+            cg.append(words)
+
+        pieces = [(0, 128), (128, 256), (256, 384), (384, 512)]
+        z_ps = []
+        for i, (lo, hi) in enumerate(pieces):
+            c_codes = keep.tile([P, PASSES, hi - lo], U16, name=f"c_codes{i}", align_bytes=64)
+            words = cg[lo // HALF][:, lo % HALF : lo % HALF + hi - lo]
+            nc.vector.tensor_copy(c_codes[:], words.bitcast(U16).rearrange("p (n o) -> p o n", o=PASSES))
+            z = psum.tile([P, hi - lo], F32, name=f"z{i}")
+            for g0 in range(0, hi - lo, GROUP):
+                product(z[:, g0 : g0 + GROUP], c_codes, cs, slice(g0, g0 + GROUP), slice(lo + g0, lo + g0 + GROUP))
+            z_ps.append(z)
 
         res = keep.tile([P, N], F32, name="res")
-        stored = 0
-        for g in range(4):
-            cols = slice(g * GROUP, (g + 1) * GROUP)
-            prod = keep.tile([P, GROUP], F32, name=f"prod{g}")
-            nc.vector.tensor_tensor(prod[:], z_ps[g][:], a_sb[:, cols], ALU.mult)
-            pos = keep.tile([P, GROUP], F32, name=f"pos{g}")
-            nc.vector.tensor_scalar(pos[:], prod[:], 0.0, 1.0, ALU.max, ALU.add)
-            nc.scalar.activation(out=res[:, cols], in_=pos[:], func=ACT.Ln)
-            if g > 0:
-                nc.sync.dma_start(out[0][:, stored : cols.stop], res[:, stored : cols.stop])
-                stored = cols.stop
+        prods = [keep.tile([P, hi - lo], F32, name=f"prod{i}") for i, (lo, hi) in enumerate(pieces)]
+
+        def multiply(i):
+            lo, hi = pieces[i]
+            nc.vector.tensor_tensor(prods[i][:], z_ps[i][:], a_sb[:, lo:hi], ALU.mult)
+
+        def finish(i):
+            lo, hi = pieces[i]
+            pos = keep.tile([P, hi - lo], F32, name=f"pos{i}")
+            nc.vector.tensor_scalar(pos[:], prods[i][:], 0.0, 1.0, ALU.max, ALU.add)
+            nc.scalar.activation(out=res[:, lo:hi], in_=pos[:], func=ACT.Ln)
+            if i > 0:
+                first = 0 if i == 1 else lo
+                nc.sync.dma_start(out[0][:, first:hi], res[:, first:hi])
+
+        multiply(0)
+        for i in range(1, len(pieces)):
+            multiply(i)
+            finish(i - 1)
+        finish(len(pieces) - 1)

@@ -34,14 +34,12 @@ def tile_attend_bilin_topk_kernel(tc, qT, k_words, k_scales, c_words, c_scales, 
         ks_win = keep.tile([P, T // 4], I32, name="ks_win", align_bytes=64)
         cs_win = keep.tile([P, T // 4], I32, name="cs_win", align_bytes=64)
         for win, scales in ((ks_win, k_scales), (cs_win, c_scales)):
-            rows = scales.rearrange("o (u v j) t -> v (o u) j t", u=2, v=2).bitcast(I32)
-            for v in range(2):
-                nc.sync.dma_start(win[48 + 32 * v : 64 + 32 * v, :], rows[v])
+            nc.scalar.dma_start(win[96:128, :], scales.rearrange("o f t -> (o f) t").bitcast(I32))
 
-        q_raw = keep.tile([P, PASSES, PACK, NQ], F32, name="q_raw", tag="q_then_ks", align_bytes=64)
-        nc.sync.dma_start(q_raw[:], qT[0].rearrange("(o p j) m -> p o j m", o=PASSES, j=PACK))
         kw_win = keep.tile([P, T], I32, name="kw_win", align_bytes=64)
         nc.sync.dma_start(kw_win[:], k_words[0].rearrange("p t b -> p (t b)").bitcast(I32))
+        q_raw = keep.tile([P, PASSES, PACK, NQ], F32, name="q_raw", align_bytes=64)
+        nc.sync.dma_start(q_raw[:], qT[0].rearrange("(o p j) m -> p o j m", o=PASSES, j=PACK))
         cw_win = keep.tile([P, T], I32, name="cw_win", align_bytes=64)
         nc.sync.dma_start(cw_win[:], c_words[0].rearrange("p t b -> p (t b)").bitcast(I32))
 
@@ -50,28 +48,25 @@ def tile_attend_bilin_topk_kernel(tc, qT, k_words, k_scales, c_words, c_scales, 
         warm = keep.tile([P, 1], F32, name="warm")
         nc.scalar.activation(out=warm[:], in_=one[:], func=ACT.Ln)
 
-        for engine, win in ((nc.vector, ks_win), (nc.gpsimd, cs_win)):
-            for lo, hi in ((0, 48), (64, 80), (96, 128)):
-                engine.memset(win[lo:hi, :], 0)
+        planes = keep.tile([P, PASSES, 2, N // 4], I32, name="planes", align_bytes=64)
+        for win in (ks_win, cs_win):
+            nc.vector.memset(win[0:96, :], 0)
+        nc.vector.memset(planes[:], 0)
+
+        picked = keep.tile([P, 2, N], U8, name="picked", align_bytes=64)
+        for tbl, win in enumerate((ks_win, cs_win)):
+            nc.vector.tensor_copy(picked[:, tbl, :], win[:].bitcast(U8).indirect(offsets[:]))
+        for o in range(PASSES):
+            for quad in range(4):
+                first = 96 + 16 * o + 4 * quad
+                queue = nc.gpsimd if (o, quad) == (0, 0) else nc.scalar
+                queue.dma_start(
+                    planes[32 * quad : 32 * quad + 4, o, :, :].rearrange("p a n -> p (a n)"),
+                    picked[first : first + 4, :, :].rearrange("p a n -> p (a n)").bitcast(I32),
+                )
 
         q_bf = keep.tile([P, PASSES, NQ, PACK], BF16, name="q_bf", align_bytes=64)
         nc.scalar.copy(out=q_bf[:], in_=q_raw[:].rearrange("p o j m -> p o m j"))
-
-        def spread(queues, plane, gathered):
-            for o in range(PASSES):
-                for u in range(2):
-                    first = 48 + 8 * o + 4 * u
-                    queues[2 * o + u].dma_start(plane[64 * u : 64 * (u + 1), o, :], gathered[first : first + 64, :].bitcast(I32))
-
-        ksg = keep.tile([P, N], U8, name="ksg", align_bytes=64)
-        nc.vector.tensor_copy(ksg[:], ks_win[:].bitcast(U8).indirect(offsets[:]))
-        ks = keep.tile([P, PASSES, N // 4], I32, name="ks", tag="q_then_ks", align_bytes=64)
-        spread([nc.scalar] * 4, ks, ksg)
-
-        csg = keep.tile([P, N], U8, name="csg", align_bytes=64)
-        nc.vector.tensor_copy(csg[:], cs_win[:].bitcast(U8).indirect(offsets[:]))
-        cs = keep.tile([P, PASSES, N // 4], I32, name="cs", align_bytes=64)
-        spread([nc.sync] * 4, cs, csg)
 
         q_codes = keep.tile([P, PASSES * NQ], U32, name="q_codes", align_bytes=64)
         q_scale = keep.tile([P, PASSES * NQ], U8, name="q_scale", align_bytes=64)
@@ -79,14 +74,14 @@ def tile_attend_bilin_topk_kernel(tc, qT, k_words, k_scales, c_words, c_scales, 
             out=q_codes[:].bitcast(FP8X4), scales=q_scale[:], in_=q_bf[:].rearrange("p o m j -> p (o m j)")
         )
 
-        def product(acc, codes, planes, cols, scols):
+        def product(acc, codes, tbl, cols, scols):
             for o in range(PASSES):
                 nc.tensor.matmul_mx(
                     out=acc,
                     lhsT=q_codes[:, o * NQ : (o + 1) * NQ].bitcast(FP8X4),
                     lhsT_scale=q_scale[:, o * NQ : (o + 1) * NQ],
                     rhs=codes[:, o, cols].bitcast(FP4X4),
-                    rhs_scale=planes[:, o, :].bitcast(U8)[:, scols],
+                    rhs_scale=planes[:, o, tbl, :].bitcast(U8)[:, scols],
                     start=(o == 0),
                     stop=(o == PASSES - 1),
                 )
@@ -100,7 +95,7 @@ def tile_attend_bilin_topk_kernel(tc, qT, k_words, k_scales, c_words, c_scales, 
             a_ps = psum.tile([P, HALF], F32, name=f"a_ps{h}")
             for g0 in range(0, HALF, GROUP):
                 cols = slice(h * HALF + g0, h * HALF + g0 + GROUP)
-                product(a_ps[:, g0 : g0 + GROUP], k_codes, ks, cols, cols)
+                product(a_ps[:, g0 : g0 + GROUP], k_codes, 0, cols, cols)
             nc.scalar.copy(out=a_sb[:, h * HALF : (h + 1) * HALF], in_=a_ps[:])
 
         cg = []
@@ -117,7 +112,7 @@ def tile_attend_bilin_topk_kernel(tc, qT, k_words, k_scales, c_words, c_scales, 
             nc.vector.tensor_copy(c_codes[:], words.bitcast(U16).rearrange("p (n o) -> p o n", o=PASSES))
             z = psum.tile([P, hi - lo], F32, name=f"z{i}")
             for g0 in range(0, hi - lo, GROUP):
-                product(z[:, g0 : g0 + GROUP], c_codes, cs, slice(g0, g0 + GROUP), slice(lo + g0, lo + g0 + GROUP))
+                product(z[:, g0 : g0 + GROUP], c_codes, 1, slice(g0, g0 + GROUP), slice(lo + g0, lo + g0 + GROUP))
             z_ps.append(z)
 
         res = keep.tile([P, N], F32, name="res")

@@ -34,14 +34,14 @@ def tile_attend_bilin_topk_kernel(tc, qT, k_words, k_scales, c_words, c_scales, 
         ks_win = keep.tile([P, T // 4], I32, name="ks_win", align_bytes=64)
         cs_win = keep.tile([P, T // 4], I32, name="cs_win", align_bytes=64)
         for win, scales in ((ks_win, k_scales), (cs_win, c_scales)):
-            nc.scalar.dma_start(win[96:128, :], scales.rearrange("o f t -> (o f) t").bitcast(I32))
+            nc.sync.dma_start(win[96:128, :], scales.rearrange("o f t -> (o f) t").bitcast(I32))
 
-        kw_win = keep.tile([P, T], I32, name="kw_win", align_bytes=64)
-        nc.sync.dma_start(kw_win[:], k_words[0].rearrange("p t b -> p (t b)").bitcast(I32))
         q_raw = keep.tile([P, PASSES, PACK, NQ], F32, name="q_raw", align_bytes=64)
-        nc.sync.dma_start(q_raw[:], qT[0].rearrange("(o p j) m -> p o j m", o=PASSES, j=PACK))
+        nc.scalar.dma_start(q_raw[:], qT[0].rearrange("(o p j) m -> p o j m", o=PASSES, j=PACK))
+        kw_win = keep.tile([P, T], I32, name="kw_win", align_bytes=64)
+        nc.scalar.dma_start(kw_win[:], k_words[0].rearrange("p t b -> p (t b)").bitcast(I32))
         cw_win = keep.tile([P, T], I32, name="cw_win", align_bytes=64)
-        nc.sync.dma_start(cw_win[:], c_words[0].rearrange("p t b -> p (t b)").bitcast(I32))
+        nc.scalar.dma_start(cw_win[:], c_words[0].rearrange("p t b -> p (t b)").bitcast(I32))
 
         one = keep.tile([P, 1], F32, name="one")
         nc.vector.memset(one[:], 1.0)
@@ -56,14 +56,14 @@ def tile_attend_bilin_topk_kernel(tc, qT, k_words, k_scales, c_words, c_scales, 
         picked = keep.tile([P, 2, N], U8, name="picked", align_bytes=64)
         for tbl, win in enumerate((ks_win, cs_win)):
             nc.vector.tensor_copy(picked[:, tbl, :], win[:].bitcast(U8).indirect(offsets[:]))
-        for o in range(PASSES):
-            for quad in range(4):
-                first = 96 + 16 * o + 4 * quad
-                queue = nc.gpsimd if (o, quad) == (0, 0) else nc.scalar
-                queue.dma_start(
-                    planes[32 * quad : 32 * quad + 4, o, :, :].rearrange("p a n -> p (a n)"),
-                    picked[first : first + 4, :, :].rearrange("p a n -> p (a n)").bitcast(I32),
-                )
+        picked_words = picked[:].rearrange("p a n -> p (a n)").bitcast(I32)
+        rows = planes[:].rearrange("p o a n -> p o (a n)")
+        for tbl in range(2):
+            cols = slice(tbl * N // 4, (tbl + 1) * N // 4)
+            nc.gpsimd.dma_start(rows[0:4, 0, cols], picked_words[96:100, cols])
+        for run in range(1, 8):
+            o, quad = divmod(run, 4)
+            nc.sync.dma_start(rows[32 * quad : 32 * quad + 4, o, :], picked_words[96 + 4 * run : 100 + 4 * run, :])
 
         q_bf = keep.tile([P, PASSES, NQ, PACK], BF16, name="q_bf", align_bytes=64)
         nc.scalar.copy(out=q_bf[:], in_=q_raw[:].rearrange("p o j m -> p o m j"))

@@ -37,11 +37,11 @@ def tile_attend_bilin_topk_kernel(tc, qT, k_words, k_scales, c_words, c_scales, 
             nc.sync.dma_start(win[96:128, :], scales.rearrange("o f t -> (o f) t").bitcast(I32))
 
         q_raw = keep.tile([P, PASSES, PACK, NQ], F32, name="q_raw", align_bytes=64)
-        nc.scalar.dma_start(q_raw[:], qT[0].rearrange("(o p j) m -> p o j m", o=PASSES, j=PACK))
+        nc.sync.dma_start(q_raw[:], qT[0].rearrange("(o p j) m -> p o j m", o=PASSES, j=PACK))
         kw_win = keep.tile([P, T], I32, name="kw_win", align_bytes=64)
-        nc.scalar.dma_start(kw_win[:], k_words[0].rearrange("p t b -> p (t b)").bitcast(I32))
+        nc.sync.dma_start(kw_win[:], k_words[0].rearrange("p t b -> p (t b)").bitcast(I32))
         cw_win = keep.tile([P, T], I32, name="cw_win", align_bytes=64)
-        nc.scalar.dma_start(cw_win[:], c_words[0].rearrange("p t b -> p (t b)").bitcast(I32))
+        nc.sync.dma_start(cw_win[:], c_words[0].rearrange("p t b -> p (t b)").bitcast(I32))
 
         one = keep.tile([P, 1], F32, name="one")
         nc.vector.memset(one[:], 1.0)
@@ -60,10 +60,12 @@ def tile_attend_bilin_topk_kernel(tc, qT, k_words, k_scales, c_words, c_scales, 
         rows = planes[:].rearrange("p o a n -> p o (a n)")
         for tbl in range(2):
             cols = slice(tbl * N // 4, (tbl + 1) * N // 4)
-            nc.gpsimd.dma_start(rows[0:4, 0, cols], picked_words[96:100, cols])
-        for run in range(1, 8):
-            o, quad = divmod(run, 4)
-            nc.sync.dma_start(rows[32 * quad : 32 * quad + 4, o, :], picked_words[96 + 4 * run : 100 + 4 * run, :])
+            nc.gpsimd.dma_start(rows[96:100, 1, cols], picked_words[124:128, cols])
+        for o in range(PASSES):
+            for quad in (0, 2, 1, 3):
+                if (o, quad) != (1, 3):
+                    first = 96 + 16 * o + 4 * quad
+                    nc.sync.dma_start(rows[32 * quad : 32 * quad + 4, o, :], picked_words[first : first + 4, :])
 
         q_bf = keep.tile([P, PASSES, NQ, PACK], BF16, name="q_bf", align_bytes=64)
         nc.scalar.copy(out=q_bf[:], in_=q_raw[:].rearrange("p o j m -> p o m j"))
@@ -91,12 +93,10 @@ def tile_attend_bilin_topk_kernel(tc, qT, k_words, k_scales, c_words, c_scales, 
         k_codes = keep.tile([P, PASSES, N], U16, name="k_codes", align_bytes=64)
         nc.vector.tensor_copy(k_codes[:], kg[:].bitcast(U16).rearrange("p (n o) -> p o n", o=PASSES))
         a_sb = keep.tile([P, N], F32, name="a_sb")
+        a_ps = psum.tile([P, N], F32, name="a_ps")
+        product(a_ps[:], k_codes, 0, slice(0, N), slice(0, N))
         for h in range(2):
-            a_ps = psum.tile([P, HALF], F32, name=f"a_ps{h}")
-            for g0 in range(0, HALF, GROUP):
-                cols = slice(h * HALF + g0, h * HALF + g0 + GROUP)
-                product(a_ps[:, g0 : g0 + GROUP], k_codes, 0, cols, cols)
-            nc.scalar.copy(out=a_sb[:, h * HALF : (h + 1) * HALF], in_=a_ps[:])
+            nc.scalar.copy(out=a_sb[:, h * HALF : (h + 1) * HALF], in_=a_ps[:, h * HALF : (h + 1) * HALF])
 
         cg = []
         for h in range(2):

@@ -93,10 +93,11 @@ def tile_attend_bilin_topk_kernel(tc, qT, k_words, k_scales, c_words, c_scales, 
         k_codes = keep.tile([P, PASSES, N], U16, name="k_codes", align_bytes=64)
         nc.vector.tensor_copy(k_codes[:], kg[:].bitcast(U16).rearrange("p (n o) -> p o n", o=PASSES))
         a_sb = keep.tile([P, N], F32, name="a_sb")
-        a_ps = psum.tile([P, N], F32, name="a_ps")
-        product(a_ps[:], k_codes, 0, slice(0, N), slice(0, N))
-        for h in range(2):
-            nc.scalar.copy(out=a_sb[:, h * HALF : (h + 1) * HALF], in_=a_ps[:, h * HALF : (h + 1) * HALF])
+        banks = [psum.tile([P, 2, GROUP], F32, name=f"bank{i}") for i in range(N // GROUP)]
+        for i, bank in enumerate(banks):
+            cols = slice(i * GROUP, (i + 1) * GROUP)
+            product(bank[:, 0, :], k_codes, 0, cols, cols)
+            nc.scalar.copy(out=a_sb[:, cols], in_=bank[:, 0, :])
 
         cg = []
         for h in range(2):
@@ -110,17 +111,15 @@ def tile_attend_bilin_topk_kernel(tc, qT, k_words, k_scales, c_words, c_scales, 
             c_codes = keep.tile([P, PASSES, hi - lo], U16, name=f"c_codes{i}", align_bytes=64)
             words = cg[lo // HALF][:, lo % HALF : lo % HALF + hi - lo]
             nc.vector.tensor_copy(c_codes[:], words.bitcast(U16).rearrange("p (n o) -> p o n", o=PASSES))
-            z = psum.tile([P, hi - lo], F32, name=f"z{i}")
-            for g0 in range(0, hi - lo, GROUP):
-                product(z[:, g0 : g0 + GROUP], c_codes, 1, slice(g0, g0 + GROUP), slice(lo + g0, lo + g0 + GROUP))
-            z_ps.append(z)
+            product(banks[i][:, 1, :], c_codes, 1, slice(0, GROUP), slice(lo, hi))
+            z_ps.append(banks[i][:, 1, :])
 
         res = keep.tile([P, N], F32, name="res")
         prods = [keep.tile([P, hi - lo], F32, name=f"prod{i}") for i, (lo, hi) in enumerate(pieces)]
 
         def multiply(i):
             lo, hi = pieces[i]
-            nc.vector.tensor_tensor(prods[i][:], z_ps[i][:], a_sb[:, lo:hi], ALU.mult)
+            nc.vector.tensor_tensor(prods[i][:], z_ps[i], a_sb[:, lo:hi], ALU.mult)
 
         def finish(i):
             lo, hi = pieces[i]

@@ -126,9 +126,8 @@ def tile_attend_bilin_topk_kernel(tc, qT, k_words, k_scales, c_words, c_scales, 
             pos = keep.tile([P, hi - lo], F32, name=f"pos{i}")
             nc.vector.tensor_scalar(pos[:], prods[i][:], 0.0, 1.0, ALU.max, ALU.add)
             nc.scalar.activation(out=res[:, lo:hi], in_=pos[:], func=ACT.Ln)
-            if i > 0:
-                first = 0 if i == 1 else lo
-                nc.sync.dma_start(out[0][:, first:hi], res[:, first:hi])
+            if hi % HALF == 0:
+                nc.sync.dma_start(out[0][:, hi - HALF : hi], res[:, hi - HALF : hi])
 
         multiply(0)
         for i in range(1, len(pieces)):

@@ -29,12 +29,12 @@ def tile_attend_bilin_topk_kernel(tc, qT, k_words, k_scales, c_words, c_scales, 
         psum = ctx.enter_context(tc.psum_pool(name="psum", bufs=1))
 
         offsets = keep.tile([P, N // 16], U16, name="offsets")
-        nc.sync.dma_start(offsets[:], offs)
 
         ks_win = keep.tile([P, T // 4], I32, name="ks_win", align_bytes=64)
         cs_win = keep.tile([P, T // 4], I32, name="cs_win", align_bytes=64)
-        for win, scales in ((ks_win, k_scales), (cs_win, c_scales)):
-            nc.sync.dma_start(win[96:128, :], scales.rearrange("o f t -> (o f) t").bitcast(I32))
+        nc.sync.dma_start(ks_win[0:32, :], k_scales.rearrange("o f t -> (o f) t").bitcast(I32))
+        nc.sync.dma_start(offsets[:], offs)
+        nc.sync.dma_start(cs_win[0:32, :], c_scales.rearrange("o f t -> (o f) t").bitcast(I32))
 
         q_raw = keep.tile([P, PASSES, PACK, NQ], F32, name="q_raw", align_bytes=64)
         nc.sync.dma_start(q_raw[:], qT[0].rearrange("(o p j) m -> p o j m", o=PASSES, j=PACK))
@@ -50,22 +50,22 @@ def tile_attend_bilin_topk_kernel(tc, qT, k_words, k_scales, c_words, c_scales, 
 
         planes = keep.tile([P, PASSES, 2, N // 4], I32, name="planes", align_bytes=64)
         for win in (ks_win, cs_win):
-            nc.vector.memset(win[0:96, :], 0)
-        nc.vector.memset(planes[:], 0)
+            nc.gpsimd.memset(win[32:64, :], 0)
+            nc.vector.memset(win[64:128, :], 0)
+        nc.gpsimd.memset(planes[:], 0)
 
         picked = keep.tile([P, 2, N], U8, name="picked", align_bytes=64)
         for tbl, win in enumerate((ks_win, cs_win)):
             nc.vector.tensor_copy(picked[:, tbl, :], win[:].bitcast(U8).indirect(offsets[:]))
         picked_words = picked[:].rearrange("p a n -> p (a n)").bitcast(I32)
         rows = planes[:].rearrange("p o a n -> p o (a n)")
-        for tbl in range(2):
-            cols = slice(tbl * N // 4, (tbl + 1) * N // 4)
-            nc.gpsimd.dma_start(rows[96:100, 1, cols], picked_words[124:128, cols])
         for o in range(PASSES):
             for quad in (0, 2, 1, 3):
-                if (o, quad) != (1, 3):
-                    first = 96 + 16 * o + 4 * quad
+                if (o, quad) != (0, 0):
+                    first = 16 * o + 4 * quad
                     nc.sync.dma_start(rows[32 * quad : 32 * quad + 4, o, :], picked_words[first : first + 4, :])
+
+        nc.vector.tensor_copy(rows[0:4, 0, :], picked_words[0:4, :])
 
         q_bf = keep.tile([P, PASSES, NQ, PACK], BF16, name="q_bf", align_bytes=64)
         nc.scalar.copy(out=q_bf[:], in_=q_raw[:].rearrange("p o j m -> p o m j"))
@@ -90,6 +90,16 @@ def tile_attend_bilin_topk_kernel(tc, qT, k_words, k_scales, c_words, c_scales, 
 
         kg = keep.tile([P, N], U32, name="kg", align_bytes=64)
         nc.vector.tensor_copy(kg[:], kw_win[:].bitcast(U32).indirect(offsets[:]))
+        spare = psum.tile([P, N], F32, name="spare")
+        nc.tensor.matmul_mx(
+            out=spare[:],
+            lhsT=q_codes[:, 0:NQ].bitcast(FP8X4),
+            lhsT_scale=q_scale[:, 0:NQ],
+            rhs=kg[:, 0 : N // 2].bitcast(FP4X4),
+            rhs_scale=picked[:, 0, :],
+            start=True,
+            stop=True,
+        )
         k_codes = keep.tile([P, PASSES, N], U16, name="k_codes", align_bytes=64)
         nc.vector.tensor_copy(k_codes[:], kg[:].bitcast(U16).rearrange("p (n o) -> p o n", o=PASSES))
         a_sb = keep.tile([P, N], F32, name="a_sb")

@@ -68,7 +68,8 @@ def tile_attend_bilin_topk_kernel(tc, qT, k_words, k_scales, c_words, c_scales, 
         nc.vector.tensor_copy(rows[0:4, 0, :], picked_words[0:4, :])
 
         q_bf = keep.tile([P, PASSES, NQ, PACK], BF16, name="q_bf", align_bytes=64)
-        nc.scalar.copy(out=q_bf[:], in_=q_raw[:].rearrange("p o j m -> p o m j"))
+        for o in range(PASSES):
+            nc.scalar.copy(out=q_bf[:, o], in_=q_raw[:, o].rearrange("p j m -> p m j"))
 
         q_codes = keep.tile([P, PASSES * NQ], U32, name="q_codes", align_bytes=64)
         q_scale = keep.tile([P, PASSES * NQ], U8, name="q_scale", align_bytes=64)
@@ -76,21 +77,21 @@ def tile_attend_bilin_topk_kernel(tc, qT, k_words, k_scales, c_words, c_scales, 
             out=q_codes[:].bitcast(FP8X4), scales=q_scale[:], in_=q_bf[:].rearrange("p o m j -> p (o m j)")
         )
 
-        def product(acc, codes, tbl, cols, scols):
-            for o in range(PASSES):
+        def product(acc, codes, tbl, cols, scols, order=(0, 1)):
+            for o in order:
                 nc.tensor.matmul_mx(
                     out=acc,
                     lhsT=q_codes[:, o * NQ : (o + 1) * NQ].bitcast(FP8X4),
                     lhsT_scale=q_scale[:, o * NQ : (o + 1) * NQ],
                     rhs=codes[:, o, cols].bitcast(FP4X4),
                     rhs_scale=planes[:, o, tbl, :].bitcast(U8)[:, scols],
-                    start=(o == 0),
-                    stop=(o == PASSES - 1),
+                    start=(o == order[0]),
+                    stop=(o == order[-1]),
                 )
 
         kg = keep.tile([P, N], U32, name="kg", align_bytes=64)
         nc.vector.tensor_copy(kg[:], kw_win[:].bitcast(U32).indirect(offsets[:]))
-        spare = psum.tile([P, N], F32, name="spare")
+        spare = psum.tile([P, N], F32, name="spare", tag="z3")
         nc.tensor.matmul_mx(
             out=spare[:],
             lhsT=q_codes[:, 0:NQ].bitcast(FP8X4),
@@ -103,11 +104,10 @@ def tile_attend_bilin_topk_kernel(tc, qT, k_words, k_scales, c_words, c_scales, 
         k_codes = keep.tile([P, PASSES, N], U16, name="k_codes", align_bytes=64)
         nc.vector.tensor_copy(k_codes[:], kg[:].bitcast(U16).rearrange("p (n o) -> p o n", o=PASSES))
         a_sb = keep.tile([P, N], F32, name="a_sb")
-        banks = [psum.tile([P, 2, GROUP], F32, name=f"bank{i}") for i in range(N // GROUP)]
-        for i, bank in enumerate(banks):
-            cols = slice(i * GROUP, (i + 1) * GROUP)
-            product(bank[:, 0, :], k_codes, 0, cols, cols)
-            nc.scalar.copy(out=a_sb[:, cols], in_=bank[:, 0, :])
+        a_bank = psum.tile([P, N], F32, name="a_bank")
+        product(a_bank[:], k_codes, 0, slice(0, N), slice(0, N))
+        for first in range(0, N, GROUP):
+            nc.scalar.copy(out=a_sb[:, first : first + GROUP], in_=a_bank[:, first : first + GROUP])
 
         cg = []
         for h in range(2):
@@ -117,12 +117,15 @@ def tile_attend_bilin_topk_kernel(tc, qT, k_words, k_scales, c_words, c_scales, 
 
         pieces = [(0, 128), (128, 256), (256, 384), (384, 512)]
         z_ps = []
-        for i, (lo, hi) in enumerate(pieces):
-            c_codes = keep.tile([P, PASSES, hi - lo], U16, name=f"c_codes{i}", align_bytes=64)
+        for lo, hi in ((0, 128), (128, 256), (256, 512)):
+            c_codes = keep.tile([P, PASSES, hi - lo], U16, name=f"c_codes{lo}", align_bytes=64)
             words = cg[lo // HALF][:, lo % HALF : lo % HALF + hi - lo]
             nc.vector.tensor_copy(c_codes[:], words.bitcast(U16).rearrange("p (n o) -> p o n", o=PASSES))
-            product(banks[i][:, 1, :], c_codes, 1, slice(0, GROUP), slice(lo, hi))
-            z_ps.append(banks[i][:, 1, :])
+            for first in range(lo, hi, GROUP):
+                i = first // GROUP
+                z_bank = psum.tile([P, GROUP], F32, name=f"z{i}", tag=f"z{i}")
+                product(z_bank[:], c_codes, 1, slice(first - lo, first - lo + GROUP), slice(first, first + GROUP), order=(1, 0))
+                z_ps.append(z_bank[:])
 
         res = keep.tile([P, N], F32, name="res")
         prods = [keep.tile([P, hi - lo], F32, name=f"prod{i}") for i, (lo, hi) in enumerate(pieces)]
@@ -134,8 +137,12 @@ def tile_attend_bilin_topk_kernel(tc, qT, k_words, k_scales, c_words, c_scales, 
         def finish(i):
             lo, hi = pieces[i]
             pos = keep.tile([P, hi - lo], F32, name=f"pos{i}")
-            nc.vector.tensor_scalar(pos[:], prods[i][:], 0.0, 1.0, ALU.max, ALU.add)
-            nc.scalar.activation(out=res[:, lo:hi], in_=pos[:], func=ACT.Ln)
+            if hi <= GROUP:
+                nc.scalar.activation(out=pos[:], in_=prods[i][:], func=ACT.Relu)
+                nc.scalar.activation(out=res[:, lo:hi], in_=pos[:], func=ACT.Ln, bias=1.0)
+            else:
+                nc.vector.tensor_scalar(pos[:], prods[i][:], 0.0, 1.0, ALU.max, ALU.add)
+                nc.scalar.activation(out=res[:, lo:hi], in_=pos[:], func=ACT.Ln)
             if hi % HALF == 0:
                 nc.sync.dma_start(out[0][:, hi - HALF : hi], res[:, hi - HALF : hi])
 

@@ -91,16 +91,6 @@ def tile_attend_bilin_topk_kernel(tc, qT, k_words, k_scales, c_words, c_scales, 
 
         kg = keep.tile([P, N], U32, name="kg", align_bytes=64)
         nc.vector.tensor_copy(kg[:], kw_win[:].bitcast(U32).indirect(offsets[:]))
-        spare = psum.tile([P, N], F32, name="spare", tag="z3")
-        nc.tensor.matmul_mx(
-            out=spare[:],
-            lhsT=q_codes[:, 0:NQ].bitcast(FP8X4),
-            lhsT_scale=q_scale[:, 0:NQ],
-            rhs=kg[:, 0 : N // 2].bitcast(FP4X4),
-            rhs_scale=picked[:, 0, :],
-            start=True,
-            stop=True,
-        )
         k_codes = keep.tile([P, PASSES, N], U16, name="k_codes", align_bytes=64)
         nc.vector.tensor_copy(k_codes[:], kg[:].bitcast(U16).rearrange("p (n o) -> p o n", o=PASSES))
         a_sb = keep.tile([P, N], F32, name="a_sb")

@@ -92,7 +92,18 @@ def tile_attend_bilin_topk_kernel(tc, qT, k_words, k_scales, c_words, c_scales, 
         kg = keep.tile([P, N], U32, name="kg", align_bytes=64)
         nc.vector.tensor_copy(kg[:], kw_win[:].bitcast(U32).indirect(offsets[:]))
         k_codes = keep.tile([P, PASSES, N], U16, name="k_codes", align_bytes=64)
-        nc.vector.tensor_copy(k_codes[:], kg[:].bitcast(U16).rearrange("p (n o) -> p o n", o=PASSES))
+        for o in range(PASSES):
+            nc.vector.tensor_copy(k_codes[:, o, :], kg[:].bitcast(U16).rearrange("p (n o) -> p o n", o=PASSES)[:, o, :])
+        idle_bank = psum.tile([P, N], F32, name="idle_bank")
+        nc.tensor.matmul_mx(
+            out=idle_bank[:],
+            lhsT=q_codes[:, :NQ].bitcast(FP8X4),
+            lhsT_scale=q_scale[:, :NQ],
+            rhs=k_codes[:, 0, :].bitcast(FP4X4),
+            rhs_scale=picked[:, 0, :],
+            start=True,
+            stop=True,
+        )
         a_sb = keep.tile([P, N], F32, name="a_sb")
         a_bank = psum.tile([P, N], F32, name="a_bank")
         product(a_bank[:], k_codes, 0, slice(0, N), slice(0, N))
@@ -107,10 +118,15 @@ def tile_attend_bilin_topk_kernel(tc, qT, k_words, k_scales, c_words, c_scales, 
 
         pieces = [(0, 128), (128, 256), (256, 384), (384, 512)]
         z_ps = []
-        for lo, hi in ((0, 128), (128, 256), (256, 512)):
+        for lo, hi in pieces:
             c_codes = keep.tile([P, PASSES, hi - lo], U16, name=f"c_codes{lo}", align_bytes=64)
             words = cg[lo // HALF][:, lo % HALF : lo % HALF + hi - lo]
-            nc.vector.tensor_copy(c_codes[:], words.bitcast(U16).rearrange("p (n o) -> p o n", o=PASSES))
+            halves = words.bitcast(U16).rearrange("p (n o) -> p o n", o=PASSES)
+            if lo == 0:
+                for o in (1, 0):
+                    nc.vector.tensor_copy(c_codes[:, o, :], halves[:, o, :])
+            else:
+                nc.vector.tensor_copy(c_codes[:], halves)
             for first in range(lo, hi, GROUP):
                 i = first // GROUP
                 z_bank = psum.tile([P, GROUP], F32, name=f"z{i}", tag=f"z{i}")

@@ -95,15 +95,16 @@ def tile_attend_bilin_topk_kernel(tc, qT, k_words, k_scales, c_words, c_scales, 
         for o in range(PASSES):
             nc.vector.tensor_copy(k_codes[:, o, :], kg[:].bitcast(U16).rearrange("p (n o) -> p o n", o=PASSES)[:, o, :])
         idle_bank = psum.tile([P, N], F32, name="idle_bank")
-        nc.tensor.matmul_mx(
-            out=idle_bank[:],
-            lhsT=q_codes[:, :NQ].bitcast(FP8X4),
-            lhsT_scale=q_scale[:, :NQ],
-            rhs=k_codes[:, 0, :].bitcast(FP4X4),
-            rhs_scale=picked[:, 0, :],
-            start=True,
-            stop=True,
-        )
+        for lo, hi in ((0, GROUP), (GROUP, GROUP + GROUP // 2)):
+            nc.tensor.matmul_mx(
+                out=idle_bank[:, lo:hi],
+                lhsT=q_codes[:, :NQ].bitcast(FP8X4),
+                lhsT_scale=q_scale[:, :NQ],
+                rhs=k_codes[:, 1, lo:hi].bitcast(FP4X4),
+                rhs_scale=picked[:, 0, lo:hi],
+                start=True,
+                stop=True,
+            )
         a_sb = keep.tile([P, N], F32, name="a_sb")
         a_bank = psum.tile([P, N], F32, name="a_bank")
         product(a_bank[:], k_codes, 0, slice(0, N), slice(0, N))
@@ -122,7 +123,7 @@ def tile_attend_bilin_topk_kernel(tc, qT, k_words, k_scales, c_words, c_scales, 
             c_codes = keep.tile([P, PASSES, hi - lo], U16, name=f"c_codes{lo}", align_bytes=64)
             words = cg[lo // HALF][:, lo % HALF : lo % HALF + hi - lo]
             halves = words.bitcast(U16).rearrange("p (n o) -> p o n", o=PASSES)
-            if lo == 0:
+            if lo in (0, N - GROUP):
                 for o in (1, 0):
                     nc.vector.tensor_copy(c_codes[:, o, :], halves[:, o, :])
             else:
@@ -134,26 +135,31 @@ def tile_attend_bilin_topk_kernel(tc, qT, k_words, k_scales, c_words, c_scales, 
                 z_ps.append(z_bank[:])
 
         res = keep.tile([P, N], F32, name="res")
-        prods = [keep.tile([P, hi - lo], F32, name=f"prod{i}") for i, (lo, hi) in enumerate(pieces)]
+        cuts = [0,128,256,384,448,512]
+        steps = list(zip(cuts, cuts[1:]))
+        store_cuts = [0,256,384,512]
+        prods = [keep.tile([P, hi - lo], F32, name=f"prod{i}") for i, (lo, hi) in enumerate(steps)]
 
         def multiply(i):
-            lo, hi = pieces[i]
-            nc.vector.tensor_tensor(prods[i][:], z_ps[i], a_sb[:, lo:hi], ALU.mult)
+            lo, hi = steps[i]
+            z_cols = z_ps[lo // GROUP][:, lo % GROUP : lo % GROUP + hi - lo]
+            nc.vector.tensor_tensor(prods[i][:], z_cols, a_sb[:, lo:hi], ALU.mult)
 
         def finish(i):
-            lo, hi = pieces[i]
+            lo, hi = steps[i]
             pos = keep.tile([P, hi - lo], F32, name=f"pos{i}")
-            if hi <= GROUP:
+            if i < 1:
                 nc.scalar.activation(out=pos[:], in_=prods[i][:], func=ACT.Relu)
                 nc.scalar.activation(out=res[:, lo:hi], in_=pos[:], func=ACT.Ln, bias=1.0)
             else:
                 nc.vector.tensor_scalar(pos[:], prods[i][:], 0.0, 1.0, ALU.max, ALU.add)
                 nc.scalar.activation(out=res[:, lo:hi], in_=pos[:], func=ACT.Ln)
-            if hi % HALF == 0:
-                nc.sync.dma_start(out[0][:, hi - HALF : hi], res[:, hi - HALF : hi])
+            if hi in store_cuts:
+                first = store_cuts[store_cuts.index(hi) - 1]
+                nc.sync.dma_start(out[0][:, first:hi], res[:, first:hi])
 
         multiply(0)
-        for i in range(1, len(pieces)):
+        for i in range(1, len(steps)):
             multiply(i)
             finish(i - 1)
-        finish(len(pieces) - 1)
+        finish(len(steps) - 1)

@@ -94,17 +94,6 @@ def tile_attend_bilin_topk_kernel(tc, qT, k_words, k_scales, c_words, c_scales, 
         k_codes = keep.tile([P, PASSES, N], U16, name="k_codes", align_bytes=64)
         for o in range(PASSES):
             nc.vector.tensor_copy(k_codes[:, o, :], kg[:].bitcast(U16).rearrange("p (n o) -> p o n", o=PASSES)[:, o, :])
-        idle_bank = psum.tile([P, N], F32, name="idle_bank")
-        for lo, hi in ((0, GROUP), (GROUP, GROUP + GROUP // 2)):
-            nc.tensor.matmul_mx(
-                out=idle_bank[:, lo:hi],
-                lhsT=q_codes[:, :NQ].bitcast(FP8X4),
-                lhsT_scale=q_scale[:, :NQ],
-                rhs=k_codes[:, 1, lo:hi].bitcast(FP4X4),
-                rhs_scale=picked[:, 0, lo:hi],
-                start=True,
-                stop=True,
-            )
         a_sb = keep.tile([P, N], F32, name="a_sb")
         a_bank = psum.tile([P, N], F32, name="a_bank")
         product(a_bank[:], k_codes, 0, slice(0, N), slice(0, N))

@@ -50,7 +50,7 @@ def tile_attend_bilin_topk_kernel(tc, qT, k_words, k_scales, c_words, c_scales, 
 
         planes = keep.tile([P, PASSES, 2, N // 4], I32, name="planes", align_bytes=64)
         for win in (ks_win, cs_win):
-            nc.gpsimd.memset(win[32:64, :], 0)
+            nc.vector.memset(win[32:64, :], 0)
             nc.vector.memset(win[64:128, :], 0)
         nc.gpsimd.memset(planes[:], 0)
 
@@ -61,11 +61,9 @@ def tile_attend_bilin_topk_kernel(tc, qT, k_words, k_scales, c_words, c_scales, 
         rows = planes[:].rearrange("p o a n -> p o (a n)")
         for o in range(PASSES):
             for quad in (0, 2, 1, 3):
-                if (o, quad) != (0, 0):
-                    first = 16 * o + 4 * quad
-                    nc.sync.dma_start(rows[32 * quad : 32 * quad + 4, o, :], picked_words[first : first + 4, :])
-
-        nc.vector.tensor_copy(rows[0:4, 0, :], picked_words[0:4, :])
+                first = 16 * o + 4 * quad
+                queue = nc.gpsimd if (o, quad) == (1, 3) else nc.sync
+                queue.dma_start(rows[32 * quad : 32 * quad + 4, o, :], picked_words[first : first + 4, :])
 
         q_bf = keep.tile([P, PASSES, NQ, PACK], BF16, name="q_bf", align_bytes=64)
         for o in range(PASSES):
@@ -92,8 +90,7 @@ def tile_attend_bilin_topk_kernel(tc, qT, k_words, k_scales, c_words, c_scales, 
         kg = keep.tile([P, N], U32, name="kg", align_bytes=64)
         nc.vector.tensor_copy(kg[:], kw_win[:].bitcast(U32).indirect(offsets[:]))
         k_codes = keep.tile([P, PASSES, N], U16, name="k_codes", align_bytes=64)
-        for o in range(PASSES):
-            nc.vector.tensor_copy(k_codes[:, o, :], kg[:].bitcast(U16).rearrange("p (n o) -> p o n", o=PASSES)[:, o, :])
+        nc.vector.tensor_copy(k_codes[:], kg[:].bitcast(U16).rearrange("p (n o) -> p o n", o=PASSES))
         a_sb = keep.tile([P, N], F32, name="a_sb")
         a_bank = psum.tile([P, N], F32, name="a_bank")
         product(a_bank[:], k_codes, 0, slice(0, N), slice(0, N))

@@ -29,101 +29,113 @@ def tile_attend_bilin_topk_kernel(tc, qT, k_words, k_scales, c_words, c_scales, 
         psum = ctx.enter_context(tc.psum_pool(name="psum", bufs=1))
 
         offsets = keep.tile([P, N // 16], U16, name="offsets")
-
         ks_win = keep.tile([P, T // 4], I32, name="ks_win", align_bytes=64)
         cs_win = keep.tile([P, T // 4], I32, name="cs_win", align_bytes=64)
-        nc.sync.dma_start(ks_win[0:32, :], k_scales.rearrange("o f t -> (o f) t").bitcast(I32))
+        nc.sync.dma_start(ks_win[0:32, :], k_scales.rearrange("o f t -> f o t").bitcast(I32))
         nc.sync.dma_start(offsets[:], offs)
-        nc.sync.dma_start(cs_win[0:32, :], c_scales.rearrange("o f t -> (o f) t").bitcast(I32))
+        nc.sync.dma_start(cs_win[64:96, :], c_scales.rearrange("o f t -> f o t").bitcast(I32))
 
-        q_raw = keep.tile([P, PASSES, PACK, NQ], F32, name="q_raw", align_bytes=64)
-        nc.sync.dma_start(q_raw[:], qT[0].rearrange("(o p j) m -> p o j m", o=PASSES, j=PACK))
-        kw_win = keep.tile([P, T], I32, name="kw_win", align_bytes=64)
+        q_rows = qT[0].rearrange("(o p j) m -> o p j m", o=PASSES, j=PACK)
+        q_raw = [keep.tile([P, PACK, NQ], F32, name=f"q_raw{o}", tag=f"q_raw{o}", align_bytes=64) for o in range(PASSES)]
+        nc.sync.dma_start(q_raw[0][:], q_rows[0])
+        kw_win = keep.tile([P, T], I32, name="kw_win", tag="kw_win", align_bytes=64)
         nc.sync.dma_start(kw_win[:], k_words[0].rearrange("p t b -> p (t b)").bitcast(I32))
-        cw_win = keep.tile([P, T], I32, name="cw_win", align_bytes=64)
-        nc.sync.dma_start(cw_win[:], c_words[0].rearrange("p t b -> p (t b)").bitcast(I32))
+        nc.sync.dma_start(q_raw[1][:], q_rows[1])
 
         one = keep.tile([P, 1], F32, name="one")
         nc.vector.memset(one[:], 1.0)
         warm = keep.tile([P, 1], F32, name="warm")
         nc.scalar.activation(out=warm[:], in_=one[:], func=ACT.Ln)
 
-        planes = keep.tile([P, PASSES, 2, N // 4], I32, name="planes", align_bytes=64)
-        for win in (ks_win, cs_win):
-            nc.vector.memset(win[32:64, :], 0)
-            nc.vector.memset(win[64:128, :], 0)
-        nc.gpsimd.memset(planes[:], 0)
+        planes = [keep.tile([P, PASSES * N // 4], I32, name="planes0", align_bytes=64)]
+        nc.gpsimd.memset(ks_win[32:64, :], 0)
+        nc.vector.memset(ks_win[64:128, :], 0)
+        nc.gpsimd.memset(planes[0][:], 0)
+        nc.vector.memset(cs_win[0:64, :], 0)
+        nc.gpsimd.memset(cs_win[96:128, :], 0)
 
-        picked = keep.tile([P, 2, N], U8, name="picked", align_bytes=64)
+        picked = []
         for tbl, win in enumerate((ks_win, cs_win)):
-            nc.vector.tensor_copy(picked[:, tbl, :], win[:].bitcast(U8).indirect(offsets[:]))
-        picked_words = picked[:].rearrange("p a n -> p (a n)").bitcast(I32)
-        rows = planes[:].rearrange("p o a n -> p o (a n)")
-        for o in range(PASSES):
-            for quad in (0, 2, 1, 3):
-                first = 16 * o + 4 * quad
-                queue = nc.gpsimd if (o, quad) == (1, 3) else nc.sync
-                queue.dma_start(rows[32 * quad : 32 * quad + 4, o, :], picked_words[first : first + 4, :])
+            picked.append(keep.tile([P, N], U8, name=f"picked{tbl}", align_bytes=64))
+            nc.vector.tensor_copy(picked[tbl][:], win[:].bitcast(U8).indirect(offsets[:]))
 
-        q_bf = keep.tile([P, PASSES, NQ, PACK], BF16, name="q_bf", align_bytes=64)
-        for o in range(PASSES):
-            nc.scalar.copy(out=q_bf[:, o], in_=q_raw[:, o].rearrange("p j m -> p m j"))
+        def move_rows(tbl, quad, queue):
+            first = 64 * tbl + 8 * quad
+            queue.dma_start(planes[tbl][32 * quad : 32 * quad + 4, :], picked[tbl][first : first + 8, :].bitcast(I32))
 
-        q_codes = keep.tile([P, PASSES * NQ], U32, name="q_codes", align_bytes=64)
-        q_scale = keep.tile([P, PASSES * NQ], U8, name="q_scale", align_bytes=64)
-        nc.vector.quantize_mx(
-            out=q_codes[:].bitcast(FP8X4), scales=q_scale[:], in_=q_bf[:].rearrange("p o m j -> p (o m j)")
-        )
+        move_rows(0, 0, nc.gpsimd)
+        for quad in (2, 1, 3):
+            move_rows(0, quad, nc.sync)
 
-        def product(acc, codes, tbl, cols, scols, order=(0, 1)):
-            for o in order:
+        q_codes = [keep.tile([P, NQ], U32, name=f"q_codes{o}", align_bytes=64) for o in range(PASSES)]
+        q_scale = [keep.tile([P, NQ], U8, name=f"q_scale{o}", align_bytes=64) for o in range(PASSES)]
+        q_bf = [keep.tile([P, NQ, PACK], BF16, name=f"q_bf{o}", tag=f"cast{o}", align_bytes=64) for o in range(PASSES)]
+
+        def quantise(o):
+            nc.vector.quantize_mx(
+                out=q_codes[o][:].bitcast(FP8X4), scales=q_scale[o][:], in_=q_bf[o][:].rearrange("p m j -> p (m j)")
+            )
+
+        nc.scalar.copy(out=q_bf[0][:], in_=q_raw[0][:].rearrange("p j m -> p m j"))
+        cw_win = keep.tile([P, T], I32, name="cw_win", tag="q_raw0", align_bytes=64)
+        nc.scalar.dma_start(cw_win[:], c_words[0].rearrange("p t b -> p (t b)").bitcast(I32))
+        quantise(0)
+
+        def product(acc, codes, tbl, first, width):
+            for o in range(PASSES):
                 nc.tensor.matmul_mx(
                     out=acc,
-                    lhsT=q_codes[:, o * NQ : (o + 1) * NQ].bitcast(FP8X4),
-                    lhsT_scale=q_scale[:, o * NQ : (o + 1) * NQ],
-                    rhs=codes[:, o, cols].bitcast(FP4X4),
-                    rhs_scale=planes[:, o, tbl, :].bitcast(U8)[:, scols],
-                    start=(o == order[0]),
-                    stop=(o == order[-1]),
+                    lhsT=q_codes[o][:].bitcast(FP8X4),
+                    lhsT_scale=q_scale[o][:],
+                    rhs=codes[o].bitcast(FP4X4),
+                    rhs_scale=planes[tbl][:].bitcast(U8)[:, o * N + first : o * N + first + width],
+                    start=(o == 0),
+                    stop=(o == PASSES - 1),
                 )
 
-        kg = keep.tile([P, N], U32, name="kg", align_bytes=64)
+        kg = keep.tile([P, N], U32, name="kg", tag="gathered", align_bytes=64)
         nc.vector.tensor_copy(kg[:], kw_win[:].bitcast(U32).indirect(offsets[:]))
-        k_codes = keep.tile([P, PASSES, N], U16, name="k_codes", align_bytes=64)
-        nc.vector.tensor_copy(k_codes[:], kg[:].bitcast(U16).rearrange("p (n o) -> p o n", o=PASSES))
+        nc.scalar.copy(out=q_bf[1][:], in_=q_raw[1][:].rearrange("p j m -> p m j"))
+        planes.append(keep.tile([P, PASSES * N // 4], I32, name="planes1", tag="kw_win", align_bytes=64))
+        nc.vector.memset(planes[1][:], 0)
+        for quad in (0, 2, 1, 3):
+            move_rows(1, quad, nc.sync)
+        k_halves = kg[:].bitcast(U16).rearrange("p (n o) -> p o n", o=PASSES)
+        k_codes = [keep.tile([P, N], U16, name="k_codes0", tag="cast0", align_bytes=64)]
+        nc.vector.tensor_copy(k_codes[0][:], k_halves[:, 0, :])
+        quantise(1)
+        k_codes.append(keep.tile([P, N], U16, name="k_codes1", tag="cast1", align_bytes=64))
+        nc.vector.tensor_copy(k_codes[1][:], k_halves[:, 1, :])
         a_sb = keep.tile([P, N], F32, name="a_sb")
         a_bank = psum.tile([P, N], F32, name="a_bank")
-        product(a_bank[:], k_codes, 0, slice(0, N), slice(0, N))
-        for first in range(0, N, GROUP):
-            nc.scalar.copy(out=a_sb[:, first : first + GROUP], in_=a_bank[:, first : first + GROUP])
+        product(a_bank[:], [k_codes[0][:], k_codes[1][:]], 0, 0, N)
+        for first in range(0, N, HALF):
+            nc.scalar.copy(out=a_sb[:, first : first + HALF], in_=a_bank[:, first : first + HALF])
 
-        cg = []
+        cg = keep.tile([P, N], U32, name="cg", tag="gathered", align_bytes=64)
         for h in range(2):
-            words = keep.tile([P, HALF], U32, name=f"cg{h}", align_bytes=64)
-            nc.vector.tensor_copy(words[:], cw_win[:].bitcast(U32).indirect(offsets[:, 16 * h : 16 * (h + 1)]))
-            cg.append(words)
+            nc.vector.tensor_copy(
+                cg[:, h * HALF : (h + 1) * HALF], cw_win[:].bitcast(U32).indirect(offsets[:, 16 * h : 16 * (h + 1)])
+            )
 
-        pieces = [(0, 128), (128, 256), (256, 384), (384, 512)]
         z_ps = []
-        for lo, hi in pieces:
-            c_codes = keep.tile([P, PASSES, hi - lo], U16, name=f"c_codes{lo}", align_bytes=64)
-            words = cg[lo // HALF][:, lo % HALF : lo % HALF + hi - lo]
+        for lo in range(0, N, GROUP):
+            c_codes = keep.tile([P, PASSES, GROUP], U16, name=f"c_codes{lo}", align_bytes=64)
+            words = cg[:, lo : lo + GROUP]
             halves = words.bitcast(U16).rearrange("p (n o) -> p o n", o=PASSES)
             if lo in (0, N - GROUP):
-                for o in (1, 0):
+                for o in range(PASSES):
                     nc.vector.tensor_copy(c_codes[:, o, :], halves[:, o, :])
             else:
                 nc.vector.tensor_copy(c_codes[:], halves)
-            for first in range(lo, hi, GROUP):
-                i = first // GROUP
-                z_bank = psum.tile([P, GROUP], F32, name=f"z{i}", tag=f"z{i}")
-                product(z_bank[:], c_codes, 1, slice(first - lo, first - lo + GROUP), slice(first, first + GROUP), order=(1, 0))
-                z_ps.append(z_bank[:])
+            z_bank = psum.tile([P, GROUP], F32, name=f"z{lo}", tag=f"z{lo}")
+            product(z_bank[:], [c_codes[:, 0, :], c_codes[:, 1, :]], 1, lo, GROUP)
+            z_ps.append(z_bank[:])
 
         res = keep.tile([P, N], F32, name="res")
-        cuts = [0,128,256,384,448,512]
+        cuts = [0, 128, 256, 384, 448, 512]
         steps = list(zip(cuts, cuts[1:]))
-        store_cuts = [0,256,384,512]
+        store_cuts = [0, 256, 512]
         prods = [keep.tile([P, hi - lo], F32, name=f"prod{i}") for i, (lo, hi) in enumerate(steps)]
 
         def multiply(i):
@@ -134,7 +146,7 @@ def tile_attend_bilin_topk_kernel(tc, qT, k_words, k_scales, c_words, c_scales, 
         def finish(i):
             lo, hi = steps[i]
             pos = keep.tile([P, hi - lo], F32, name=f"pos{i}")
-            if i < 1:
+            if i < 2:
                 nc.scalar.activation(out=pos[:], in_=prods[i][:], func=ACT.Relu)
                 nc.scalar.activation(out=res[:, lo:hi], in_=pos[:], func=ACT.Ln, bias=1.0)
             else:

@@ -29,83 +29,64 @@ def tile_attend_bilin_topk_kernel(tc, qT, k_words, k_scales, c_words, c_scales, 
         psum = ctx.enter_context(tc.psum_pool(name="psum", bufs=1))
 
         offsets = keep.tile([P, N // 16], U16, name="offsets")
-        ks_win = keep.tile([P, T // 4], I32, name="ks_win", align_bytes=64)
+        ks_win = keep.tile([P, T // 4], I32, name="ks_win", tag="ks_then_cw", align_bytes=64)
         cs_win = keep.tile([P, T // 4], I32, name="cs_win", align_bytes=64)
         nc.sync.dma_start(ks_win[0:32, :], k_scales.rearrange("o f t -> f o t").bitcast(I32))
         nc.sync.dma_start(offsets[:], offs)
-        nc.sync.dma_start(cs_win[64:96, :], c_scales.rearrange("o f t -> f o t").bitcast(I32))
+        nc.sync.dma_start(cs_win[0:32, :], c_scales.rearrange("o f t -> f o t").bitcast(I32))
 
-        q_rows = qT[0].rearrange("(o p j) m -> o p j m", o=PASSES, j=PACK)
-        q_raw = [keep.tile([P, PACK, NQ], F32, name=f"q_raw{o}", tag=f"q_raw{o}", align_bytes=64) for o in range(PASSES)]
-        nc.sync.dma_start(q_raw[0][:], q_rows[0])
-        kw_win = keep.tile([P, T], I32, name="kw_win", tag="kw_win", align_bytes=64)
+        q_raw = keep.tile([P, PASSES, PACK, NQ], F32, name="q_raw", align_bytes=64)
+        nc.sync.dma_start(q_raw[:], qT[0].rearrange("(o p j) m -> p o j m", o=PASSES, j=PACK))
+        kw_win = keep.tile([P, T], I32, name="kw_win", align_bytes=64)
         nc.sync.dma_start(kw_win[:], k_words[0].rearrange("p t b -> p (t b)").bitcast(I32))
-        nc.sync.dma_start(q_raw[1][:], q_rows[1])
 
         one = keep.tile([P, 1], F32, name="one")
         nc.vector.memset(one[:], 1.0)
         warm = keep.tile([P, 1], F32, name="warm")
         nc.scalar.activation(out=warm[:], in_=one[:], func=ACT.Ln)
 
-        planes = [keep.tile([P, PASSES * N // 4], I32, name="planes0", align_bytes=64)]
-        nc.gpsimd.memset(ks_win[32:64, :], 0)
-        nc.vector.memset(ks_win[64:128, :], 0)
-        nc.gpsimd.memset(planes[0][:], 0)
-        nc.vector.memset(cs_win[0:64, :], 0)
-        nc.gpsimd.memset(cs_win[96:128, :], 0)
+        planes = keep.tile([P, PASSES * 2 * N // 4], I32, name="planes", align_bytes=64)
+        for win in (ks_win, cs_win):
+            nc.gpsimd.memset(win[32:64, :], 0)
+            nc.vector.memset(win[64:128, :], 0)
+        nc.gpsimd.memset(planes[:], 0)
 
-        picked = []
+        picked = keep.tile([P, 2 * N], U8, name="picked", align_bytes=64)
         for tbl, win in enumerate((ks_win, cs_win)):
-            picked.append(keep.tile([P, N], U8, name=f"picked{tbl}", align_bytes=64))
-            nc.vector.tensor_copy(picked[tbl][:], win[:].bitcast(U8).indirect(offsets[:]))
+            nc.vector.tensor_copy(picked[:, tbl * N : (tbl + 1) * N], win[:].bitcast(U8).indirect(offsets[:]))
+        for quad in (0, 2, 1, 3):
+            nc.sync.dma_start(planes[32 * quad : 32 * quad + 4, :], picked[8 * quad : 8 * quad + 8, :].bitcast(I32))
 
-        def move_rows(tbl, quad, queue):
-            first = 64 * tbl + 8 * quad
-            queue.dma_start(planes[tbl][32 * quad : 32 * quad + 4, :], picked[tbl][first : first + 8, :].bitcast(I32))
-
-        move_rows(0, 0, nc.gpsimd)
-        for quad in (2, 1, 3):
-            move_rows(0, quad, nc.sync)
-
-        q_codes = [keep.tile([P, NQ], U32, name=f"q_codes{o}", align_bytes=64) for o in range(PASSES)]
-        q_scale = [keep.tile([P, NQ], U8, name=f"q_scale{o}", align_bytes=64) for o in range(PASSES)]
-        q_bf = [keep.tile([P, NQ, PACK], BF16, name=f"q_bf{o}", tag=f"cast{o}", align_bytes=64) for o in range(PASSES)]
-
-        def quantise(o):
-            nc.vector.quantize_mx(
-                out=q_codes[o][:].bitcast(FP8X4), scales=q_scale[o][:], in_=q_bf[o][:].rearrange("p m j -> p (m j)")
-            )
-
-        nc.scalar.copy(out=q_bf[0][:], in_=q_raw[0][:].rearrange("p j m -> p m j"))
-        cw_win = keep.tile([P, T], I32, name="cw_win", tag="q_raw0", align_bytes=64)
+        cw_win = keep.tile([P, T], I32, name="cw_win", tag="ks_then_cw", align_bytes=64)
         nc.scalar.dma_start(cw_win[:], c_words[0].rearrange("p t b -> p (t b)").bitcast(I32))
-        quantise(0)
+
+        q_bf = keep.tile([P, PASSES, NQ, PACK], BF16, name="q_bf", align_bytes=64)
+        for o in range(PASSES):
+            nc.scalar.copy(out=q_bf[:, o], in_=q_raw[:, o].rearrange("p j m -> p m j"))
+        q_codes = keep.tile([P, PASSES * NQ], U32, name="q_codes", align_bytes=64)
+        q_scale = keep.tile([P, PASSES * NQ], U8, name="q_scale", align_bytes=64)
+        nc.vector.quantize_mx(
+            out=q_codes[:].bitcast(FP8X4), scales=q_scale[:], in_=q_bf[:].rearrange("p o m j -> p (o m j)")
+        )
 
         def product(acc, codes, tbl, first, width):
             for o in range(PASSES):
                 nc.tensor.matmul_mx(
                     out=acc,
-                    lhsT=q_codes[o][:].bitcast(FP8X4),
-                    lhsT_scale=q_scale[o][:],
+                    lhsT=q_codes[:, o * NQ : (o + 1) * NQ].bitcast(FP8X4),
+                    lhsT_scale=q_scale[:, o * NQ : (o + 1) * NQ],
                     rhs=codes[o].bitcast(FP4X4),
-                    rhs_scale=planes[tbl][:].bitcast(U8)[:, o * N + first : o * N + first + width],
+                    rhs_scale=planes[:].bitcast(U8)[:, (2 * o + tbl) * N + first : (2 * o + tbl) * N + first + width],
                     start=(o == 0),
                     stop=(o == PASSES - 1),
                 )
 
         kg = keep.tile([P, N], U32, name="kg", tag="gathered", align_bytes=64)
         nc.vector.tensor_copy(kg[:], kw_win[:].bitcast(U32).indirect(offsets[:]))
-        nc.scalar.copy(out=q_bf[1][:], in_=q_raw[1][:].rearrange("p j m -> p m j"))
-        planes.append(keep.tile([P, PASSES * N // 4], I32, name="planes1", tag="kw_win", align_bytes=64))
-        nc.vector.memset(planes[1][:], 0)
-        for quad in (0, 2, 1, 3):
-            move_rows(1, quad, nc.sync)
         k_halves = kg[:].bitcast(U16).rearrange("p (n o) -> p o n", o=PASSES)
-        k_codes = [keep.tile([P, N], U16, name="k_codes0", tag="cast0", align_bytes=64)]
-        nc.vector.tensor_copy(k_codes[0][:], k_halves[:, 0, :])
-        quantise(1)
-        k_codes.append(keep.tile([P, N], U16, name="k_codes1", tag="cast1", align_bytes=64))
-        nc.vector.tensor_copy(k_codes[1][:], k_halves[:, 1, :])
+        k_codes = [keep.tile([P, N], U16, name=f"k_codes{o}", align_bytes=64) for o in range(PASSES)]
+        for o in range(PASSES):
+            nc.vector.tensor_copy(k_codes[o][:], k_halves[:, o, :])
         a_sb = keep.tile([P, N], F32, name="a_sb")
         a_bank = psum.tile([P, N], F32, name="a_bank")
         product(a_bank[:], [k_codes[0][:], k_codes[1][:]], 0, 0, N)
@@ -135,7 +116,7 @@ def tile_attend_bilin_topk_kernel(tc, qT, k_words, k_scales, c_words, c_scales, 
         res = keep.tile([P, N], F32, name="res")
         cuts = [0, 128, 256, 384, 448, 512]
         steps = list(zip(cuts, cuts[1:]))
-        store_cuts = [0, 256, 512]
+        store_cuts = [0, 256, 384, 512]
         prods = [keep.tile([P, hi - lo], F32, name=f"prod{i}") for i, (lo, hi) in enumerate(steps)]
 
         def multiply(i):

from contextlib import ExitStack

import concourse.mybir as mybir

F32 = mybir.dt.float32
BF16 = mybir.dt.bfloat16
I32 = mybir.dt.int32
U32 = mybir.dt.uint32
U16 = mybir.dt.uint16
U8 = mybir.dt.uint8
FP8X4 = mybir.dt.float8_e4m3fn_x4
FP4X4 = mybir.dt.float4_e2m1fn_x4
ALU = mybir.AluOpType
ACT = mybir.ActivationFunctionType

P = 128
N, T, D, NQ = 512, 2048, 1024, 128
PASSES = 2
PACK = 4
HALF = N // 2
GROUP = 128
FLOPS = 2 * 2 * NQ * N * D


def tile_attend_bilin_topk_kernel(tc, qT, k_words, k_scales, c_words, c_scales, offs, out):
    nc = tc.nc
    with ExitStack() as ctx:
        keep = ctx.enter_context(tc.tile_pool(name="keep", bufs=1))
        psum = ctx.enter_context(tc.psum_pool(name="psum", bufs=1))

        offsets = keep.tile([P, N // 16], U16, name="offsets")
        ks_win = keep.tile([P, T // 4], I32, name="ks_win", tag="ks_then_cw", align_bytes=64)
        cs_win = keep.tile([P, T // 4], I32, name="cs_win", align_bytes=64)
        nc.sync.dma_start(ks_win[0:32, :], k_scales.rearrange("o f t -> f o t").bitcast(I32))
        nc.sync.dma_start(offsets[:], offs)
        nc.sync.dma_start(cs_win[0:32, :], c_scales.rearrange("o f t -> f o t").bitcast(I32))

        q_raw = keep.tile([P, PASSES, PACK, NQ], F32, name="q_raw", align_bytes=64)
        nc.sync.dma_start(q_raw[:], qT[0].rearrange("(o p j) m -> p o j m", o=PASSES, j=PACK))
        kw_win = keep.tile([P, T], I32, name="kw_win", align_bytes=64)
        nc.sync.dma_start(kw_win[:], k_words[0].rearrange("p t b -> p (t b)").bitcast(I32))

        one = keep.tile([P, 1], F32, name="one")
        nc.vector.memset(one[:], 1.0)
        warm = keep.tile([P, 1], F32, name="warm")
        nc.scalar.activation(out=warm[:], in_=one[:], func=ACT.Ln)

        planes = keep.tile([P, PASSES * 2 * N // 4], I32, name="planes", align_bytes=64)
        for win in (ks_win, cs_win):
            nc.gpsimd.memset(win[32:64, :], 0)
            nc.vector.memset(win[64:128, :], 0)
        nc.gpsimd.memset(planes[:], 0)

        picked = keep.tile([P, 2 * N], U8, name="picked", align_bytes=64)
        for tbl, win in enumerate((ks_win, cs_win)):
            nc.vector.tensor_copy(picked[:, tbl * N : (tbl + 1) * N], win[:].bitcast(U8).indirect(offsets[:]))
        for quad in (0, 2, 1, 3):
            nc.sync.dma_start(planes[32 * quad : 32 * quad + 4, :], picked[8 * quad : 8 * quad + 8, :].bitcast(I32))

        cw_win = keep.tile([P, T], I32, name="cw_win", tag="ks_then_cw", align_bytes=64)
        nc.scalar.dma_start(cw_win[:], c_words[0].rearrange("p t b -> p (t b)").bitcast(I32))

        q_bf = keep.tile([P, PASSES, NQ, PACK], BF16, name="q_bf", align_bytes=64)
        for o in range(PASSES):
            nc.scalar.copy(out=q_bf[:, o], in_=q_raw[:, o].rearrange("p j m -> p m j"))
        q_codes = keep.tile([P, PASSES * NQ], U32, name="q_codes", align_bytes=64)
        q_scale = keep.tile([P, PASSES * NQ], U8, name="q_scale", align_bytes=64)
        nc.vector.quantize_mx(
            out=q_codes[:].bitcast(FP8X4), scales=q_scale[:], in_=q_bf[:].rearrange("p o m j -> p (o m j)")
        )

        def product(acc, codes, tbl, first, width):
            for o in range(PASSES):
                nc.tensor.matmul_mx(
                    out=acc,
                    lhsT=q_codes[:, o * NQ : (o + 1) * NQ].bitcast(FP8X4),
                    lhsT_scale=q_scale[:, o * NQ : (o + 1) * NQ],
                    rhs=codes[o].bitcast(FP4X4),
                    rhs_scale=planes[:].bitcast(U8)[:, (2 * o + tbl) * N + first : (2 * o + tbl) * N + first + width],
                    start=(o == 0),
                    stop=(o == PASSES - 1),
                )

        kg = keep.tile([P, N], U32, name="kg", tag="gathered", align_bytes=64)
        nc.vector.tensor_copy(kg[:], kw_win[:].bitcast(U32).indirect(offsets[:]))
        k_halves = kg[:].bitcast(U16).rearrange("p (n o) -> p o n", o=PASSES)
        k_codes = [keep.tile([P, N], U16, name=f"k_codes{o}", align_bytes=64) for o in range(PASSES)]
        for o in range(PASSES):
            nc.vector.tensor_copy(k_codes[o][:], k_halves[:, o, :])
        a_sb = keep.tile([P, N], F32, name="a_sb")
        a_bank = psum.tile([P, N], F32, name="a_bank")
        product(a_bank[:], [k_codes[0][:], k_codes[1][:]], 0, 0, N)
        for first in range(0, N, HALF):
            nc.scalar.copy(out=a_sb[:, first : first + HALF], in_=a_bank[:, first : first + HALF])

        cg = keep.tile([P, N], U32, name="cg", tag="gathered", align_bytes=64)
        for h in range(2):
            nc.vector.tensor_copy(
                cg[:, h * HALF : (h + 1) * HALF], cw_win[:].bitcast(U32).indirect(offsets[:, 16 * h : 16 * (h + 1)])
            )

        z_ps = []
        for lo in range(0, N, GROUP):
            c_codes = keep.tile([P, PASSES, GROUP], U16, name=f"c_codes{lo}", align_bytes=64)
            words = cg[:, lo : lo + GROUP]
            halves = words.bitcast(U16).rearrange("p (n o) -> p o n", o=PASSES)
            if lo in (0, N - GROUP):
                for o in range(PASSES):
                    nc.vector.tensor_copy(c_codes[:, o, :], halves[:, o, :])
            else:
                nc.vector.tensor_copy(c_codes[:], halves)
            z_bank = psum.tile([P, GROUP], F32, name=f"z{lo}", tag=f"z{lo}")
            product(z_bank[:], [c_codes[:, 0, :], c_codes[:, 1, :]], 1, lo, GROUP)
            z_ps.append(z_bank[:])

        res = keep.tile([P, N], F32, name="res")
        cuts = [0, 128, 256, 384, 448, 512]
        steps = list(zip(cuts, cuts[1:]))
        store_cuts = [0, 256, 384, 512]
        prods = [keep.tile([P, hi - lo], F32, name=f"prod{i}") for i, (lo, hi) in enumerate(steps)]

        def multiply(i):
            lo, hi = steps[i]
            z_cols = z_ps[lo // GROUP][:, lo % GROUP : lo % GROUP + hi - lo]
            nc.vector.tensor_tensor(prods[i][:], z_cols, a_sb[:, lo:hi], ALU.mult)

        def finish(i):
            lo, hi = steps[i]
            pos = keep.tile([P, hi - lo], F32, name=f"pos{i}")
            if i < 2:
                nc.scalar.activation(out=pos[:], in_=prods[i][:], func=ACT.Relu)
                nc.scalar.activation(out=res[:, lo:hi], in_=pos[:], func=ACT.Ln, bias=1.0)
            else:
                nc.vector.tensor_scalar(pos[:], prods[i][:], 0.0, 1.0, ALU.max, ALU.add)
                nc.scalar.activation(out=res[:, lo:hi], in_=pos[:], func=ACT.Ln)
            if hi in store_cuts:
                first = store_cuts[store_cuts.index(hi) - 1]
                nc.sync.dma_start(out[0][:, first:hi], res[:, first:hi])

        multiply(0)
        for i in range(1, len(steps)):
            multiply(i)
            finish(i - 1)
        finish(len(steps) - 1)
